import numpy as np
import ml_dtypes

BF16 = ml_dtypes.bfloat16


def bf(x):
    return np.asarray(x, np.float32).astype(BF16)


def f32(x):
    return np.asarray(x, np.float32)


def f64(x):
    return np.asarray(x).astype(np.float64)


def striped(idx):
    return np.tile(idx.reshape(-1, 16).T, (8, 1))


S, K, M, N = 512, 128, 256, 192


def setup_inputs():
    return {"base": bf(np.random.standard_normal((M, S))), "x": bf(np.random.standard_normal((K, N))), "w": bf(np.random.standard_normal((K, M)) / np.sqrt(K)), "b": f32(0.5 * np.random.standard_normal((M, 1))), "offs": striped(np.random.permutation(S)[:N])}


def reference(base, x, w, b, offs):
    idx = offs[:16].T.reshape(-1)
    z = f64(base).copy()
    z[:, idx] = f64(w).T @ f64(x)
    return np.tanh(z + f64(b))

@@ -1,0 +1,63 @@
+import concourse.mybir as mybir
+from concourse.masks import make_identity
+
+P = 128
+S = 512
+N = 192
+M = 256
+BLOCKS = M // P
+
+FLOPS = 2 * P * M * N
+
+BF16 = mybir.dt.bfloat16
+F32 = mybir.dt.float32
+U16 = mybir.dt.uint16
+TANH = mybir.ActivationFunctionType.Tanh
+
+
+def tile_scatter_matmul_kernel(tc, base, x, w, b, offs, out):
+    nc = tc.nc
+    with (
+        tc.tile_pool(name="held", bufs=1) as held,
+        tc.psum_pool(name="windows", bufs=1) as windows,
+    ):
+        offsets = held.tile([P, N // 16], U16, name="offsets")
+        nc.sync.dma_start(offsets[:], offs)
+
+        base_tiles = []
+        for a in range(BLOCKS):
+            base_tile = held.tile([P, S], BF16, name="base%d" % a)
+            nc.sync.dma_start(base_tile[:], base[a * P : (a + 1) * P, :])
+            base_tiles.append(base_tile)
+
+        w_tile = held.tile([P, M], BF16, name="w_tile")
+        nc.scalar.dma_start(w_tile[:], w)
+        x_tile = held.tile([P, N], BF16, name="x_tile")
+        nc.scalar.dma_start(x_tile[:], x)
+        bias_tile = held.tile([P, BLOCKS], F32, name="bias_tile")
+        nc.scalar.dma_start(bias_tile[:], b.rearrange("(a p) o -> p (a o)", p=P))
+
+        identity = held.tile([P, P], BF16, name="identity")
+        make_identity(nc, identity[:])
+
+        window_tiles = []
+        for a in range(BLOCKS):
+            window = windows.tile([P, S], F32, name="window%d" % a)
+            nc.tensor.matmul(window[:], identity[:], base_tiles[a][:], start=True, stop=True)
+            window_tiles.append(window)
+
+        for a in range(BLOCKS):
+            nc.tensor.matmul(
+                window_tiles[a][:].indirect(offsets[:]),
+                w_tile[:, a * P : (a + 1) * P],
+                x_tile[:],
+                start=True,
+                stop=True,
+            )
+
+        for a in range(BLOCKS):
+            result = held.tile([P, S], F32, name="result%d" % a)
+            nc.scalar.activation(
+                result[:], window_tiles[a][:], TANH, bias=bias_tile[:, a : a + 1]
+            )
+            nc.sync.dma_start(out[a * P : (a + 1) * P, :], result[:])

@@ -24,18 +24,23 @@ def tile_scatter_matmul_kernel(tc, base, x, w, b, offs, out):
         offsets = held.tile([P, N // 16], U16, name="offsets")
         nc.sync.dma_start(offsets[:], offs)
 
+        load_queues = [nc.scalar, nc.sync]
         base_tiles = []
         for a in range(BLOCKS):
             base_tile = held.tile([P, S], BF16, name="base%d" % a)
-            nc.sync.dma_start(base_tile[:], base[a * P : (a + 1) * P, :])
+            load_queues[a].dma_start(base_tile[:], base[a * P : (a + 1) * P, :])
             base_tiles.append(base_tile)
 
         w_tile = held.tile([P, M], BF16, name="w_tile")
         nc.scalar.dma_start(w_tile[:], w)
         x_tile = held.tile([P, N], BF16, name="x_tile")
-        nc.scalar.dma_start(x_tile[:], x)
+        nc.sync.dma_start(x_tile[:], x)
         bias_tile = held.tile([P, BLOCKS], F32, name="bias_tile")
         nc.scalar.dma_start(bias_tile[:], b.rearrange("(a p) o -> p (a o)", p=P))
+
+        table_warmer = held.tile([P, 1], F32, name="table_warmer")
+        nc.vector.memset(table_warmer[:], 0.0)
+        nc.scalar.activation(table_warmer[:], table_warmer[:], TANH)
 
         identity = held.tile([P, P], BF16, name="identity")
         make_identity(nc, identity[:])

@@ -7,6 +7,8 @@ N = 192
 M = 256
 BLOCKS = M // P
 
+WARM_MATMULS = 3
+
 FLOPS = 2 * P * M * N
 
 BF16 = mybir.dt.bfloat16
@@ -38,9 +40,15 @@ def tile_scatter_matmul_kernel(tc, base, x, w, b, offs, out):
         bias_tile = held.tile([P, BLOCKS], F32, name="bias_tile")
         nc.scalar.dma_start(bias_tile[:], b.rearrange("(a p) o -> p (a o)", p=P))
 
+        zeros = held.tile([P, S], BF16, name="zeros")
+        nc.gpsimd.memset(zeros[:].bitcast(F32), 0.0)
+
         table_warmer = held.tile([P, 1], F32, name="table_warmer")
-        nc.vector.memset(table_warmer[:], 0.0)
-        nc.scalar.activation(table_warmer[:], table_warmer[:], TANH)
+        nc.scalar.activation(table_warmer[:], zeros[:, 0:1], TANH)
+
+        unread = windows.tile([P, S], F32, name="unread")
+        for i in range(WARM_MATMULS):
+            nc.tensor.matmul(unread[:], zeros[:, 0:P], zeros[:], start=True, stop=True)
 
         identity = held.tile([P, P], BF16, name="identity")
         make_identity(nc, identity[:])

@@ -23,22 +23,21 @@ def tile_scatter_matmul_kernel(tc, base, x, w, b, offs, out):
         tc.tile_pool(name="held", bufs=1) as held,
         tc.psum_pool(name="windows", bufs=1) as windows,
     ):
-        offsets = held.tile([P, N // 16], U16, name="offsets")
-        nc.sync.dma_start(offsets[:], offs)
-
-        load_queues = [nc.scalar, nc.sync]
         base_tiles = []
         for a in range(BLOCKS):
             base_tile = held.tile([P, S], BF16, name="base%d" % a)
-            load_queues[a].dma_start(base_tile[:], base[a * P : (a + 1) * P, :])
+            nc.sync.dma_start(base_tile[:], base[a * P : (a + 1) * P, :])
             base_tiles.append(base_tile)
 
+        offsets = held.tile([P, N // 16], U16, name="offsets")
+        nc.sync.dma_start(offsets[:], offs)
+
         w_tile = held.tile([P, M], BF16, name="w_tile")
-        nc.scalar.dma_start(w_tile[:], w)
+        nc.sync.dma_start(w_tile[:], w)
         x_tile = held.tile([P, N], BF16, name="x_tile")
         nc.sync.dma_start(x_tile[:], x)
         bias_tile = held.tile([P, BLOCKS], F32, name="bias_tile")
-        nc.scalar.dma_start(bias_tile[:], b.rearrange("(a p) o -> p (a o)", p=P))
+        nc.sync.dma_start(bias_tile[:], b.rearrange("(a p) o -> p (a o)", p=P))
 
         zeros = held.tile([P, S], BF16, name="zeros")
         nc.gpsimd.memset(zeros[:].bitcast(F32), 0.0)

@@ -7,7 +7,7 @@ N = 192
 M = 256
 BLOCKS = M // P
 
-WARM_MATMULS = 3
+WARM_MATMULS = 2
 
 FLOPS = 2 * P * M * N
 

@@ -39,18 +39,25 @@ def tile_scatter_matmul_kernel(tc, base, x, w, b, offs, out):
         bias_tile = held.tile([P, BLOCKS], F32, name="bias_tile")
         nc.sync.dma_start(bias_tile[:], b.rearrange("(a p) o -> p (a o)", p=P))
 
-        zeros = held.tile([P, S], BF16, name="zeros")
-        nc.gpsimd.memset(zeros[:].bitcast(F32), 0.0)
+        identity = held.tile([P, P], BF16, name="identity")
+        make_identity(nc, identity[:])
+
+        zeros = held.tile([P, P], BF16, name="zeros")
+        nc.vector.memset(zeros[:].bitcast(F32), 0.0)
 
         table_warmer = held.tile([P, 1], F32, name="table_warmer")
         nc.scalar.activation(table_warmer[:], zeros[:, 0:1], TANH)
 
         unread = windows.tile([P, S], F32, name="unread")
+        zeros_repeated = zeros[:].unsqueeze(1).to_broadcast([P, S // P, P])
         for i in range(WARM_MATMULS):
-            nc.tensor.matmul(unread[:], zeros[:, 0:P], zeros[:], start=True, stop=True)
-
-        identity = held.tile([P, P], BF16, name="identity")
-        make_identity(nc, identity[:])
+            nc.tensor.matmul(
+                unread[:].rearrange("p (r c) -> p r c", c=P),
+                zeros[:],
+                zeros_repeated,
+                start=True,
+                stop=True,
+            )
 
         window_tiles = []
         for a in range(BLOCKS):

@@ -8,6 +8,7 @@ M = 256
 BLOCKS = M // P
 
 WARM_MATMULS = 2
+DMA_GRID = 256
 
 FLOPS = 2 * P * M * N
 
@@ -25,16 +26,16 @@ def tile_scatter_matmul_kernel(tc, base, x, w, b, offs, out):
     ):
         base_tiles = []
         for a in range(BLOCKS):
-            base_tile = held.tile([P, S], BF16, name="base%d" % a)
+            base_tile = held.tile([P, S], BF16, name="base%d" % a, align_bytes=DMA_GRID)
             nc.sync.dma_start(base_tile[:], base[a * P : (a + 1) * P, :])
             base_tiles.append(base_tile)
 
         offsets = held.tile([P, N // 16], U16, name="offsets")
         nc.sync.dma_start(offsets[:], offs)
 
-        w_tile = held.tile([P, M], BF16, name="w_tile")
+        w_tile = held.tile([P, M], BF16, name="w_tile", align_bytes=DMA_GRID)
         nc.sync.dma_start(w_tile[:], w)
-        x_tile = held.tile([P, N], BF16, name="x_tile")
+        x_tile = held.tile([P, N], BF16, name="x_tile", align_bytes=DMA_GRID)
         nc.sync.dma_start(x_tile[:], x)
         bias_tile = held.tile([P, BLOCKS], F32, name="bias_tile")
         nc.sync.dma_start(bias_tile[:], b.rearrange("(a p) o -> p (a o)", p=P))
@@ -75,7 +76,7 @@ def tile_scatter_matmul_kernel(tc, base, x, w, b, offs, out):
             )
 
         for a in range(BLOCKS):
-            result = held.tile([P, S], F32, name="result%d" % a)
+            result = held.tile([P, S], F32, name="result%d" % a, align_bytes=DMA_GRID)
             nc.scalar.activation(
                 result[:], window_tiles[a][:], TANH, bias=bias_tile[:, a : a + 1]
             )

@@ -30,15 +30,17 @@ def tile_scatter_matmul_kernel(tc, base, x, w, b, offs, out):
             nc.sync.dma_start(base_tile[:], base[a * P : (a + 1) * P, :])
             base_tiles.append(base_tile)
 
-        offsets = held.tile([P, N // 16], U16, name="offsets")
+        offsets = held.tile([P, N // 16], U16, name="offsets", align_bytes=DMA_GRID)
         nc.sync.dma_start(offsets[:], offs)
 
         w_tile = held.tile([P, M], BF16, name="w_tile", align_bytes=DMA_GRID)
         nc.sync.dma_start(w_tile[:], w)
         x_tile = held.tile([P, N], BF16, name="x_tile", align_bytes=DMA_GRID)
         nc.sync.dma_start(x_tile[:], x)
-        bias_tile = held.tile([P, BLOCKS], F32, name="bias_tile")
-        nc.sync.dma_start(bias_tile[:], b.rearrange("(a p) o -> p (a o)", p=P))
+        bias_tile = held.tile(
+            [P, BLOCKS, DMA_GRID // 4], F32, name="bias_tile", align_bytes=DMA_GRID
+        )
+        nc.sync.dma_start(bias_tile[:, :, 0:1], b.rearrange("(a p) o -> p a o", p=P))
 
         identity = held.tile([P, P], BF16, name="identity")
         make_identity(nc, identity[:])
@@ -78,6 +80,6 @@ def tile_scatter_matmul_kernel(tc, base, x, w, b, offs, out):
         for a in range(BLOCKS):
             result = held.tile([P, S], F32, name="result%d" % a, align_bytes=DMA_GRID)
             nc.scalar.activation(
-                result[:], window_tiles[a][:], TANH, bias=bias_tile[:, a : a + 1]
+                result[:], window_tiles[a][:], TANH, bias=bias_tile[:, a, 0:1]
             )
             nc.sync.dma_start(out[a * P : (a + 1) * P, :], result[:])

@@ -7,6 +7,9 @@ N = 192
 M = 256
 BLOCKS = M // P
 
+GROUP = 32
+PIECE = 88
+
 WARM_MATMULS = 2
 DMA_GRID = 256
 
@@ -26,9 +29,10 @@ def tile_scatter_matmul_kernel(tc, base, x, w, b, offs, out):
     ):
         base_tiles = []
         for a in range(BLOCKS):
-            base_tile = held.tile([P, S], BF16, name="base%d" % a, align_bytes=DMA_GRID)
-            nc.sync.dma_start(base_tile[:], base[a * P : (a + 1) * P, :])
-            base_tiles.append(base_tile)
+            base_tiles.append(
+                held.tile([P, S], BF16, name="base%d" % a, align_bytes=DMA_GRID)
+            )
+        nc.sync.dma_start(base_tiles[0][:], base[0:P, :])
 
         offsets = held.tile([P, N // 16], U16, name="offsets", align_bytes=DMA_GRID)
         nc.sync.dma_start(offsets[:], offs)
@@ -41,6 +45,7 @@ def tile_scatter_matmul_kernel(tc, base, x, w, b, offs, out):
             [P, BLOCKS, DMA_GRID // 4], F32, name="bias_tile", align_bytes=DMA_GRID
         )
         nc.sync.dma_start(bias_tile[:, :, 0:1], b.rearrange("(a p) o -> p a o", p=P))
+        nc.sync.dma_start(base_tiles[1][:], base[P:M, :])
 
         identity = held.tile([P, P], BF16, name="identity")
         make_identity(nc, identity[:])
@@ -65,17 +70,27 @@ def tile_scatter_matmul_kernel(tc, base, x, w, b, offs, out):
         window_tiles = []
         for a in range(BLOCKS):
             window = windows.tile([P, S], F32, name="window%d" % a)
-            nc.tensor.matmul(window[:], identity[:], base_tiles[a][:], start=True, stop=True)
-            window_tiles.append(window)
-
-        for a in range(BLOCKS):
+            if a == 0:
+                nc.tensor.matmul(window[:], identity[:], base_tiles[a][:], start=True, stop=True)
+            else:
+                for c in range(0, S, PIECE):
+                    columns = slice(c, min(c + PIECE, S))
+                    for g in range(0, P, GROUP):
+                        nc.tensor.matmul(
+                            window[g : g + GROUP, columns],
+                            identity[:, g : g + GROUP],
+                            base_tiles[a][:, columns],
+                            start=True,
+                            stop=True,
+                        )
             nc.tensor.matmul(
-                window_tiles[a][:].indirect(offsets[:]),
+                window[:].indirect(offsets[:]),
                 w_tile[:, a * P : (a + 1) * P],
                 x_tile[:],
                 start=True,
                 stop=True,
             )
+            window_tiles.append(window)
 
         for a in range(BLOCKS):
             result = held.tile([P, S], F32, name="result%d" % a, align_bytes=DMA_GRID)

@@ -41,11 +41,11 @@ def tile_scatter_matmul_kernel(tc, base, x, w, b, offs, out):
         nc.sync.dma_start(w_tile[:], w)
         x_tile = held.tile([P, N], BF16, name="x_tile", align_bytes=DMA_GRID)
         nc.sync.dma_start(x_tile[:], x)
+        nc.sync.dma_start(base_tiles[1][:], base[P:M, :])
         bias_tile = held.tile(
             [P, BLOCKS, DMA_GRID // 4], F32, name="bias_tile", align_bytes=DMA_GRID
         )
         nc.sync.dma_start(bias_tile[:, :, 0:1], b.rearrange("(a p) o -> p a o", p=P))
-        nc.sync.dma_start(base_tiles[1][:], base[P:M, :])
 
         identity = held.tile([P, P], BF16, name="identity")
         make_identity(nc, identity[:])

@@ -10,7 +10,7 @@ BLOCKS = M // P
 GROUP = 32
 PIECE = 88
 
-WARM_MATMULS = 2
+WARM_ROUNDS = 2
 DMA_GRID = 256
 
 FLOPS = 2 * P * M * N
@@ -50,22 +50,23 @@ def tile_scatter_matmul_kernel(tc, base, x, w, b, offs, out):
         identity = held.tile([P, P], BF16, name="identity")
         make_identity(nc, identity[:])
 
-        zeros = held.tile([P, P], BF16, name="zeros")
+        zeros = held.tile([P, GROUP], BF16, name="zeros")
         nc.vector.memset(zeros[:].bitcast(F32), 0.0)
 
         table_warmer = held.tile([P, 1], F32, name="table_warmer")
         nc.scalar.activation(table_warmer[:], zeros[:, 0:1], TANH)
 
         unread = windows.tile([P, S], F32, name="unread")
-        zeros_repeated = zeros[:].unsqueeze(1).to_broadcast([P, S // P, P])
-        for i in range(WARM_MATMULS):
-            nc.tensor.matmul(
-                unread[:].rearrange("p (r c) -> p r c", c=P),
-                zeros[:],
-                zeros_repeated,
-                start=True,
-                stop=True,
-            )
+        zeros_repeated = zeros[:].unsqueeze(1).to_broadcast([P, S // GROUP, GROUP])
+        for i in range(WARM_ROUNDS):
+            for g in range(0, P, GROUP):
+                nc.tensor.matmul(
+                    unread[g : g + GROUP, :].rearrange("p (r c) -> p r c", c=GROUP),
+                    zeros[:],
+                    zeros_repeated,
+                    start=True,
+                    stop=True,
+                )
 
         window_tiles = []
         for a in range(BLOCKS):

import concourse.mybir as mybir
from concourse.masks import make_identity

P = 128
S = 512
N = 192
M = 256
BLOCKS = M // P

GROUP = 32
PIECE = 88

WARM_ROUNDS = 2
DMA_GRID = 256

FLOPS = 2 * P * M * N

BF16 = mybir.dt.bfloat16
F32 = mybir.dt.float32
U16 = mybir.dt.uint16
TANH = mybir.ActivationFunctionType.Tanh


def tile_scatter_matmul_kernel(tc, base, x, w, b, offs, out):
    nc = tc.nc
    with (
        tc.tile_pool(name="held", bufs=1) as held,
        tc.psum_pool(name="windows", bufs=1) as windows,
    ):
        base_tiles = []
        for a in range(BLOCKS):
            base_tiles.append(
                held.tile([P, S], BF16, name="base%d" % a, align_bytes=DMA_GRID)
            )
        nc.sync.dma_start(base_tiles[0][:], base[0:P, :])

        offsets = held.tile([P, N // 16], U16, name="offsets", align_bytes=DMA_GRID)
        nc.sync.dma_start(offsets[:], offs)

        w_tile = held.tile([P, M], BF16, name="w_tile", align_bytes=DMA_GRID)
        nc.sync.dma_start(w_tile[:], w)
        x_tile = held.tile([P, N], BF16, name="x_tile", align_bytes=DMA_GRID)
        nc.sync.dma_start(x_tile[:], x)
        nc.sync.dma_start(base_tiles[1][:], base[P:M, :])
        bias_tile = held.tile(
            [P, BLOCKS, DMA_GRID // 4], F32, name="bias_tile", align_bytes=DMA_GRID
        )
        nc.sync.dma_start(bias_tile[:, :, 0:1], b.rearrange("(a p) o -> p a o", p=P))

        identity = held.tile([P, P], BF16, name="identity")
        make_identity(nc, identity[:])

        zeros = held.tile([P, GROUP], BF16, name="zeros")
        nc.vector.memset(zeros[:].bitcast(F32), 0.0)

        table_warmer = held.tile([P, 1], F32, name="table_warmer")
        nc.scalar.activation(table_warmer[:], zeros[:, 0:1], TANH)

        unread = windows.tile([P, S], F32, name="unread")
        zeros_repeated = zeros[:].unsqueeze(1).to_broadcast([P, S // GROUP, GROUP])
        for i in range(WARM_ROUNDS):
            for g in range(0, P, GROUP):
                nc.tensor.matmul(
                    unread[g : g + GROUP, :].rearrange("p (r c) -> p r c", c=GROUP),
                    zeros[:],
                    zeros_repeated,
                    start=True,
                    stop=True,
                )

        window_tiles = []
        for a in range(BLOCKS):
            window = windows.tile([P, S], F32, name="window%d" % a)
            if a == 0:
                nc.tensor.matmul(window[:], identity[:], base_tiles[a][:], start=True, stop=True)
            else:
                for c in range(0, S, PIECE):
                    columns = slice(c, min(c + PIECE, S))
                    for g in range(0, P, GROUP):
                        nc.tensor.matmul(
                            window[g : g + GROUP, columns],
                            identity[:, g : g + GROUP],
                            base_tiles[a][:, columns],
                            start=True,
                            stop=True,
                        )
            nc.tensor.matmul(
                window[:].indirect(offsets[:]),
                w_tile[:, a * P : (a + 1) * P],
                x_tile[:],
                start=True,
                stop=True,
            )
            window_tiles.append(window)

        for a in range(BLOCKS):
            result = held.tile([P, S], F32, name="result%d" % a, align_bytes=DMA_GRID)
            nc.scalar.activation(
                result[:], window_tiles[a][:], TANH, bias=bias_tile[:, a, 0:1]
            )
            nc.sync.dma_start(out[a * P : (a + 1) * P, :], result[:])
